import numpy as np
import ml_dtypes


def mxq(x, axis, fmt="e4m3"):
    dtype, down = {"e4m3": (ml_dtypes.float8_e4m3fn, 7), "e5m2": (ml_dtypes.float8_e5m2, 14)}[fmt]
    v = np.moveaxis(np.asarray(x, np.float32).astype(ml_dtypes.bfloat16).astype(np.float64), axis, -1)
    blocks = v.reshape(v.shape[:-1] + (-1, 32))
    amax = np.abs(blocks).max(-1, keepdims=True)
    byte = np.maximum(np.where(amax > 0, np.frexp(amax)[1] - 1 + 127, 0) - down, 1)
    scale = np.exp2(byte - 127.0)
    codes = (blocks / scale).astype(np.float32).astype(dtype).astype(np.float64)
    return np.moveaxis((codes * scale).reshape(v.shape), -1, axis)


WIDE = False


def mx_kscale(k):
    if not WIDE:
        return np.ones(k)
    levels = np.array([10, -10, 5, -5, 0])
    if k % 512:
        return np.exp2(np.random.permutation(np.resize(levels, k // 32))).repeat(32)
    a = np.empty((k // 512, 16))
    for p in range(k // 512):
        a[p, :8] = np.random.permutation(np.resize(levels, 8))
        for g in range(8):
            far = levels[np.abs(levels - a[p, g]) >= 10]
            a[p, g + 8] = far[np.random.randint(len(far))]
    return np.exp2(a.ravel()).repeat(32)


def f64(x):
    return np.asarray(x).astype(np.float64)


def striped(idx):
    return np.tile(np.asarray(idx).reshape(-1, 16).T, (8, 1)).astype(np.uint16)


def unstriped(offs):
    return offs[:16].T.reshape(-1).astype(np.int64)


def striped8(idx):
    return np.asarray(idx).reshape(8, -1, 16).transpose(0, 2, 1).reshape(128, -1).astype(np.uint16)


def unstriped8(offs):
    return offs.reshape(8, 16, -1).transpose(0, 2, 1).reshape(8, -1).astype(np.int64)


def pick8(x, idx, run):
    r = np.arange(len(x))
    return x[r[:, None], idx[r % (8 * run) // run]]


E2M1 = np.array([0.0, 0.5, 1.0, 1.5, 2.0, 3.0, 4.0, 6.0, -0.0, -0.5, -1.0, -1.5, -2.0, -3.0, -4.0, -6.0])


def pack_weight(w, fmt):
    k, n = w.shape
    w = f64(np.asarray(w, np.float32).astype(ml_dtypes.bfloat16)).reshape(k // 32, 32, n)
    amax = np.abs(w).max(1)
    if fmt == "e4m3":
        byte = np.frexp(amax)[1] - 1 + 127 - 7
    else:
        mant, ex = np.frexp(amax / 6.0)
        byte = np.where(mant > 0.5, ex, ex - 1) + 127
    byte = np.clip(np.where(amax > 0, byte, 1), 1, 254)
    scaled = (w * np.exp2(127.0 - byte)[:, None, :]).reshape(k, n).astype(np.float32)
    by_word = np.ascontiguousarray(scaled.reshape(k // 512, 128, 4, n).transpose(0, 1, 3, 2))
    if fmt == "e4m3":
        words = by_word.astype(ml_dtypes.float8_e4m3fn).view(np.uint8)
    else:
        c = by_word.astype(ml_dtypes.float4_e2m1fn).view(np.uint8) & 0xF
        words = (c[..., 0::2] | (c[..., 1::2] << 4)).reshape(k // 512, 128, 2 * n)
    return np.ascontiguousarray(words), np.ascontiguousarray(byte.astype(np.uint8).reshape(k // 512, 16, n))


def unpack_weight(words, scales, fmt):
    g, _, n = scales.shape
    words = np.ascontiguousarray(words).reshape(g, 128, n, -1)
    if fmt == "e4m3":
        vals = words.view(ml_dtypes.float8_e4m3fn).astype(np.float64)
    else:
        nib = np.empty((g, 128, n, 4), np.uint8)
        nib[..., 0::2] = words & 0xF
        nib[..., 1::2] = words >> 4
        vals = E2M1[nib]
    vals = vals * np.repeat(np.exp2(scales.astype(np.float64) - 127.0), 8, axis=1)[..., None]
    return vals.transpose(0, 1, 3, 2).reshape(g * 512, n)


K, J, R, T, U, O, C, N, S = 512, 256, 512, 512, 512, 128, 512, 256, 1024


def setup_inputs():
    n = np.random.standard_normal
    idx = np.stack([np.random.permutation(T)[:J] for _ in range(8)])
    idx2 = np.stack([np.random.permutation(U)[:J] for _ in range(8)])
    idx3 = np.stack([np.random.permutation(U)[:J] for _ in range(8)])
    idx4 = np.stack([np.random.permutation(C)[:J] for _ in range(8)])
    idx5 = np.stack([np.random.permutation(C)[:O] for _ in range(8)])
    idx6 = np.stack([np.random.permutation(C)[:O] for _ in range(8)])
    idx7 = np.random.permutation(S)[:N]
    fk = mx_kscale(K)
    fr = mx_kscale(R)
    wp = pack_weight(n((K, R)) * 1 / np.sqrt(K) / fk[:, None] * fr, "e2m1")
    vsp = pack_weight(n((R, S)) * 1 / np.sqrt(R) / fr[:, None], "e4m3")
    return {
        "ta": (np.random.randint(-7, 8, (K, T)).astype(np.float64)).astype(np.float32),
        "tb": (np.random.randint(-7, 8, (K, U)).astype(np.float64)).astype(np.float32),
        "ga": ((np.random.randint(8, 25, (K, 1)) / 64.0) * fk[:, None]).astype(np.float32),
        "gb": ((np.random.randint(8, 25, (K, 1)) / 64.0) * fk[:, None]).astype(np.float32),
        "gd": ((np.random.randint(8, 25, (K, 1)) / 64.0) * fk[:, None]).astype(np.float32),
        "w_words": wp[0],
        "w_scales": wp[1],
        "sa": (np.random.uniform(0.5, 1.6, (R, 1))).astype(np.float32),
        "sb": (np.random.uniform(0.5, 1.6, (R, 1))).astype(np.float32),
        "vs_words": vsp[0],
        "vs_scales": vsp[1],
        "offs": striped8(idx),
        "offs2": striped8(idx2),
        "offs3": striped8(idx3),
        "offs4": striped8(idx4),
        "offs5": striped8(idx5),
        "offs6": striped8(idx6),
        "offs7": striped(idx7),
    }


def reference(ta, tb, ga, gb, gd, w_words, w_scales, sa, sb, vs_words, vs_scales, offs, offs2, offs3, offs4, offs5, offs6, offs7):
    idx = unstriped8(offs)
    idx2 = unstriped8(offs2)
    idx3 = unstriped8(offs3)
    idx4 = unstriped8(offs4)
    idx5 = unstriped8(offs5)
    idx6 = unstriped8(offs6)
    idx7 = unstriped(offs7)
    wu = unpack_weight(w_words, w_scales, "e2m1")
    vsu = unpack_weight(vs_words, vs_scales, "e4m3")
    xc = np.maximum(np.minimum(pick8(f64(ta), idx, 64) * f64(ga), pick8(f64(tb), idx2, 64) * f64(gb)), pick8(f64(tb), idx3, 64) * f64(gd))
    xcq = mxq(xc, 0, "e4m3")
    a = wu.T @ xcq
    pw = np.zeros((R, C))
    pw[np.arange(R)[:, None], idx4[np.arange(R) % 512 // 64]] = a
    hid = np.abs(pick8(pw, idx5, 64) * f64(sa) - pick8(pw, idx6, 64) * f64(sb))
    vsidx7g = vsu[:, idx7]
    hidq = mxq(hid, 0, "e4m3")
    y = vsidx7g.T @ hidq
    return y

@@ -1,0 +1,214 @@
+from contextlib import ExitStack
+
+import concourse.mybir as mybir
+
+FLOPS = 167772160
+
+F32 = mybir.dt.float32
+BF16 = mybir.dt.bfloat16
+I32 = mybir.dt.int32
+U32 = mybir.dt.uint32
+U16 = mybir.dt.uint16
+U8 = mybir.dt.uint8
+FP8X4 = mybir.dt.float8_e4m3fn_x4
+FP4X4 = mybir.dt.float4_e2m1fn_x4
+ALU = mybir.AluOpType
+COPY = mybir.ActivationFunctionType.Copy
+
+P = 128
+PACK = 4
+LAST = PACK - 1
+TABLE = 512
+HALF = 128
+LIST_COLS = HALF // 16
+BOARD = 512
+PLACES = 128
+HIDDEN = 512
+STORE = 1024
+OUT_ROWS = 256
+RUN = 4
+
+
+def tile_picked_boundedcode_plain_one_boardpair_store_plain_kernel(
+    tc, ta, tb, ga, gb, gd, w_words, w_scales, sa, sb, vs_words, vs_scales,
+    offs, offs2, offs3, offs4, offs5, offs6, offs7, out,
+):
+    nc = tc.nc
+    with ExitStack() as ctx:
+        lists = ctx.enter_context(tc.tile_pool(name="lists", bufs=1))
+        keep = ctx.enter_context(tc.tile_pool(name="keep", bufs=1))
+        psum = ctx.enter_context(tc.psum_pool(name="psum", bufs=1))
+
+        def load_list(src, name):
+            tile = lists.tile(list(src.shape), U16, name=name)
+            nc.sync.dma_start(tile[:], src)
+            return tile
+
+        def load_factor(src, name):
+            tile = keep.tile([P, PACK], F32, name=name)
+            nc.sync.dma_start(tile[:], src.rearrange("(p t) o -> p (t o)", t=PACK))
+            return tile
+
+        def load_rows(src, t, name):
+            tile = keep.tile([P, TABLE], F32, name=name)
+            nc.sync.dma_start(tile[:], src.rearrange("(p t) c -> t p c", t=PACK)[t])
+            return tile
+
+        def load_scale_plane(src, width, name):
+            staged = keep.tile([PACK, PACK, width // 4], I32, name=name + "_staged")
+            nc.gpsimd.dma_start(staged[:], src[0].bitcast(I32).rearrange("(q i) c -> i q c", i=PACK))
+            plane = keep.tile([P, width], U8, name=name, align_bytes=64)
+            nc.vector.memset(plane[:].bitcast(I32), 0)
+            for q in range(PACK):
+                nc.vector.tensor_copy(plane[:].bitcast(I32)[32 * q : 32 * q + PACK, :], staged[:, q, :])
+            return plane
+
+        ta_rows = [load_rows(ta, 0, "ta0")]
+        list_a = load_list(offs, "list_a")
+        step_a = load_factor(ga, "step_a")
+        tb_rows = [load_rows(tb, 0, "tb0")]
+        list_upper = load_list(offs2, "list_upper")
+        step_upper = load_factor(gb, "step_upper")
+        list_lower = load_list(offs3, "list_lower")
+        step_lower = load_factor(gd, "step_lower")
+        ta_rows.append(load_rows(ta, 1, "ta1"))
+        tb_rows.append(load_rows(tb, 1, "tb1"))
+        w_raw = keep.tile([P, 2 * HIDDEN], U8, name="w_raw")
+        nc.sync.dma_start(w_raw[:].bitcast(I32), w_words[0].bitcast(I32))
+        list_store = load_list(offs7, "list_store")
+        for t in range(2, PACK):
+            ta_rows.append(load_rows(ta, t, "ta%d" % t))
+            tb_rows.append(load_rows(tb, t, "tb%d" % t))
+        list_board = load_list(offs4, "list_board")
+        vs_table = keep.tile([P, STORE], I32, name="vs_table")
+        nc.sync.dma_start(vs_table[:], vs_words[0].rearrange("p n t -> p (n t)").bitcast(I32))
+        list_first = load_list(offs5, "list_first")
+        weight_first = load_factor(sa, "weight_first")
+        list_second = load_list(offs6, "list_second")
+        weight_second = load_factor(sb, "weight_second")
+
+        w_plane = load_scale_plane(w_scales, HIDDEN, "w_plane")
+        vs_plane = load_scale_plane(vs_scales, STORE, "vs_plane")
+
+        board = [keep.tile([P, BOARD], F32, name="board%d" % t) for t in range(PACK)]
+        for t in range(PACK):
+            nc.vector.memset(board[t][:], 0.0)
+
+        w_dealt = keep.tile([P, 2 * HIDDEN], U8, name="w_dealt", align_bytes=64)
+        nc.vector.tensor_copy(
+            w_dealt[:].bitcast(U16).rearrange("p (t m) -> p t m", t=PACK),
+            w_raw[:].bitcast(U16).rearrange("p (m t) -> p t m", t=PACK),
+        )
+        w_plane_dealt = keep.tile([P, HIDDEN], U8, name="w_plane_dealt", align_bytes=64)
+        nc.vector.tensor_copy(
+            w_plane_dealt[:].rearrange("p (t m) -> p t m", t=PACK),
+            w_plane[:].rearrange("p (m t) -> p t m", t=PACK),
+        )
+        vs_plane_picked = keep.tile([P, OUT_ROWS], U8, name="vs_plane_picked", align_bytes=64)
+        nc.vector.tensor_copy(vs_plane_picked[:], vs_plane[:].indirect(list_store[:]))
+
+        def by_runs(rows):
+            return rows.rearrange("p t (c i) -> p c t i", i=RUN)
+
+        for half in range(2):
+            cols = slice(half * LIST_COLS, (half + 1) * LIST_COLS)
+            code = keep.tile([P, PACK, HALF], F32, name="code%d" % half, tag="code")
+            upper = keep.tile([P, PACK, HALF], F32, name="upper%d" % half, tag="upper")
+            lower = keep.tile([P, PACK, HALF], F32, name="lower%d" % half, tag="lower")
+            gathers = [(t, kind) for t in range(PACK) for kind in range(3)]
+            if half == 1:
+                gathers = [(t, kind) for kind in range(3) for t in range(PACK)]
+            for t, kind in gathers:
+                dst, rows, offsets, step = [
+                    (code, ta_rows, list_a, step_a),
+                    (upper, tb_rows, list_upper, step_upper),
+                    (lower, tb_rows, list_lower, step_lower),
+                ][kind]
+                nc.scalar.activation(
+                    out=dst[:, t, :], in_=rows[t][:].indirect(offsets[:, cols]), func=COPY, scale=step[:, t : t + 1]
+                )
+
+            capped = keep.tile([P, PACK, HALF], F32, name="capped%d" % half, tag="capped0" if half == 0 else "hidden0", align_bytes=64)
+            xc = keep.tile([P, HALF, PACK], BF16, name="xc%d" % half, tag="xc", align_bytes=64)
+            xc_runs = xc[:].rearrange("p (c i) t -> p c t i", i=RUN)
+            if half == 0:
+                nc.vector.tensor_tensor(capped[:, :LAST, :], code[:, :LAST, :], upper[:, :LAST, :], ALU.min)
+                nc.vector.tensor_tensor(
+                    xc_runs[:, :, :LAST, :], by_runs(capped[:, :LAST, :]), by_runs(lower[:, :LAST, :]), ALU.max
+                )
+                nc.vector.tensor_tensor(capped[:, LAST, :], code[:, LAST, :], upper[:, LAST, :], ALU.min)
+                nc.vector.tensor_tensor(xc[:, :, LAST], capped[:, LAST, :], lower[:, LAST, :], ALU.max)
+            else:
+                nc.vector.tensor_tensor(capped[:], code[:], upper[:], ALU.min)
+                nc.vector.tensor_tensor(xc_runs, by_runs(capped[:]), by_runs(lower[:]), ALU.max)
+
+            xc_words = keep.tile([P, HALF], U32, name="xc_words%d" % half, align_bytes=64)
+            xc_plane = keep.tile([P, HALF], U8, name="xc_plane%d" % half, align_bytes=64)
+            nc.vector.quantize_mx(
+                out=xc_words[:].bitcast(FP8X4), scales=xc_plane[:], in_=xc[:].rearrange("p j t -> p (j t)")
+            )
+
+            first_bank = psum.tile([P, HALF], F32, name="first_bank%d" % half)
+            rest_bank = psum.tile([P, LAST, HALF], F32, name="rest_bank%d" % half)
+            for t in range(PACK):
+                nc.tensor.matmul_mx(
+                    out=first_bank[:] if t == 0 else rest_bank[:, t - 1, :],
+                    lhsT=w_dealt[:, 2 * P * t : 2 * P * (t + 1)].bitcast(FP4X4),
+                    lhsT_scale=w_plane_dealt[:, P * t : P * (t + 1)],
+                    rhs=xc_words[:].bitcast(FP8X4),
+                    rhs_scale=xc_plane[:],
+                    start=True,
+                    stop=True,
+                )
+            hidden = keep.tile([P, PACK, HALF], F32, name="hidden%d" % half, tag="hidden%d" % half, align_bytes=64)
+            if half == 0:
+                nc.vector.tensor_copy(hidden[:, 0, :], first_bank[:])
+            else:
+                nc.scalar.copy(hidden[:, 0, :], first_bank[:])
+            nc.scalar.copy(hidden[:, 1:, :], rest_bank[:])
+            for t in range(PACK):
+                nc.vector.tensor_copy(board[t][:].indirect(list_board[:, cols]), hidden[:, t, :])
+
+        vs_picked = keep.tile([P, OUT_ROWS], U32, name="vs_picked", tag="xc", align_bytes=64)
+        nc.vector.tensor_copy(vs_picked[:], vs_table[:].bitcast(U32).indirect(list_store[:]))
+
+        first = keep.tile([P, PACK, PLACES], F32, name="first")
+        second = keep.tile([P, PACK, PLACES], F32, name="second")
+        for t in range(PACK):
+            nc.scalar.activation(
+                out=first[:, t, :], in_=board[t][:].indirect(list_first[:]), func=COPY, scale=weight_first[:, t : t + 1]
+            )
+            nc.scalar.activation(
+                out=second[:, t, :], in_=board[t][:].indirect(list_second[:]), func=COPY, scale=weight_second[:, t : t + 1]
+            )
+        gap = keep.tile([P, PACK, PLACES], F32, name="gap")
+        hid = keep.tile([P, PLACES, PACK], BF16, name="hid", align_bytes=64)
+        for rows in (slice(0, LAST), slice(LAST, PACK)):
+            nc.vector.tensor_tensor(gap[:, rows, :], first[:, rows, :], second[:, rows, :], ALU.subtract)
+            gap_by_place = gap[:, rows, :].rearrange("p t o -> p o t")
+            nc.vector.scalar_tensor_tensor(hid[:, :, rows], gap_by_place, -1.0, gap_by_place, ALU.mult, ALU.max)
+        hid_words = keep.tile([P, PLACES], U32, name="hid_words", align_bytes=64)
+        hid_plane = keep.tile([P, PLACES], U8, name="hid_plane", align_bytes=64)
+        nc.vector.quantize_mx(
+            out=hid_words[:].bitcast(FP8X4), scales=hid_plane[:], in_=hid[:].rearrange("p o t -> p (o t)")
+        )
+
+        for b in range(OUT_ROWS // P):
+            rows = slice(b * P, (b + 1) * P)
+            bank = psum.tile([P, PLACES], F32, name="out_bank%d" % b)
+            nc.tensor.matmul_mx(
+                out=bank[:],
+                lhsT=vs_picked[:, rows].bitcast(FP8X4),
+                lhsT_scale=vs_plane_picked[:, rows],
+                rhs=hid_words[:].bitcast(FP8X4),
+                rhs_scale=hid_plane[:],
+                start=True,
+                stop=True,
+            )
+            result = keep.tile([P, PLACES], F32, name="result%d" % b)
+            if b == 0:
+                nc.scalar.copy(result[:], bank[:])
+                nc.scalar.dma_start(out[rows, :], result[:])
+            else:
+                nc.vector.tensor_copy(result[:], bank[:])
+                nc.sync.dma_start(out[rows, :], result[:])

@@ -14,6 +14,7 @@ FP8X4 = mybir.dt.float8_e4m3fn_x4
 FP4X4 = mybir.dt.float4_e2m1fn_x4
 ALU = mybir.AluOpType
 COPY = mybir.ActivationFunctionType.Copy
+ABS = mybir.ActivationFunctionType.Abs
 
 P = 128
 PACK = 4
@@ -56,39 +57,50 @@ def tile_picked_boundedcode_plain_one_boardpair_store_plain_kernel(
 
         def load_scale_plane(src, width, name):
             staged = keep.tile([PACK, PACK, width // 4], I32, name=name + "_staged")
-            nc.gpsimd.dma_start(staged[:], src[0].bitcast(I32).rearrange("(q i) c -> i q c", i=PACK))
+            nc.sync.dma_start(staged[:], src[0].bitcast(I32).rearrange("(q i) c -> i q c", i=PACK))
             plane = keep.tile([P, width], U8, name=name, align_bytes=64)
             nc.vector.memset(plane[:].bitcast(I32), 0)
             for q in range(PACK):
                 nc.vector.tensor_copy(plane[:].bitcast(I32)[32 * q : 32 * q + PACK, :], staged[:, q, :])
             return plane
 
+        warm_in = keep.tile([P, 1], F32, name="warm_in")
+        warm_out = keep.tile([P, 1], F32, name="warm_out")
+        nc.vector.memset(warm_in[:], 0.0)
+        nc.scalar.activation(out=warm_out[:], in_=warm_in[:], func=COPY)
+
+        vs_plane = keep.tile([P, STORE], U8, name="vs_plane", align_bytes=64)
+        nc.vector.memset(vs_plane[:].bitcast(I32), 0)
         ta_rows = [load_rows(ta, 0, "ta0")]
         list_a = load_list(offs, "list_a")
         step_a = load_factor(ga, "step_a")
-        tb_rows = [load_rows(tb, 0, "tb0")]
         list_upper = load_list(offs2, "list_upper")
         step_upper = load_factor(gb, "step_upper")
-        list_lower = load_list(offs3, "list_lower")
-        step_lower = load_factor(gd, "step_lower")
+        tb_rows = [load_rows(tb, 0, "tb0")]
         ta_rows.append(load_rows(ta, 1, "ta1"))
         tb_rows.append(load_rows(tb, 1, "tb1"))
+        list_lower = load_list(offs3, "list_lower")
+        step_lower = load_factor(gd, "step_lower")
+        w_plane = load_scale_plane(w_scales, HIDDEN, "w_plane")
+        ta_rows.append(load_rows(ta, 2, "ta2"))
+        tb_rows.append(load_rows(tb, 2, "tb2"))
         w_raw = keep.tile([P, 2 * HIDDEN], U8, name="w_raw")
         nc.sync.dma_start(w_raw[:].bitcast(I32), w_words[0].bitcast(I32))
+        ta_rows.append(load_rows(ta, 3, "ta3"))
+        tb_rows.append(load_rows(tb, 3, "tb3"))
         list_store = load_list(offs7, "list_store")
-        for t in range(2, PACK):
-            ta_rows.append(load_rows(ta, t, "ta%d" % t))
-            tb_rows.append(load_rows(tb, t, "tb%d" % t))
-        list_board = load_list(offs4, "list_board")
-        vs_table = keep.tile([P, STORE], I32, name="vs_table")
+        vs_table = keep.tile([P, STORE], I32, name="vs_table", tag="vs_table", align_bytes=64)
         nc.sync.dma_start(vs_table[:], vs_words[0].rearrange("p n t -> p (n t)").bitcast(I32))
+        for q in range(PACK):
+            nc.sync.dma_start(
+                vs_plane[:].bitcast(I32)[32 * q : 32 * q + PACK, :], vs_scales[0].bitcast(I32)[PACK * q : PACK * (q + 1), :]
+            )
         list_first = load_list(offs5, "list_first")
         weight_first = load_factor(sa, "weight_first")
         list_second = load_list(offs6, "list_second")
         weight_second = load_factor(sb, "weight_second")
+        list_board = load_list(offs4, "list_board")
 
-        w_plane = load_scale_plane(w_scales, HIDDEN, "w_plane")
-        vs_plane = load_scale_plane(vs_scales, STORE, "vs_plane")
 
         board = [keep.tile([P, BOARD], F32, name="board%d" % t) for t in range(PACK)]
         for t in range(PACK):
@@ -104,49 +116,61 @@ def tile_picked_boundedcode_plain_one_boardpair_store_plain_kernel(
             w_plane_dealt[:].rearrange("p (t m) -> p t m", t=PACK),
             w_plane[:].rearrange("p (m t) -> p t m", t=PACK),
         )
-        vs_plane_picked = keep.tile([P, OUT_ROWS], U8, name="vs_plane_picked", align_bytes=64)
-        nc.vector.tensor_copy(vs_plane_picked[:], vs_plane[:].indirect(list_store[:]))
 
         def by_runs(rows):
             return rows.rearrange("p t (c i) -> p c t i", i=RUN)
 
+        def gather(dst, kind, t, cols):
+            rows, offsets, step = [
+                (ta_rows, list_a, step_a),
+                (tb_rows, list_upper, step_upper),
+                (tb_rows, list_lower, step_lower),
+            ][kind]
+            nc.scalar.activation(
+                out=dst, in_=rows[t][:].indirect(offsets[:, cols]), func=COPY, scale=step[:, t : t + 1]
+            )
+
+        xc = [keep.tile([P, HALF, PACK], BF16, name="xc%d" % half, align_bytes=64) for half in range(2)]
+
+        def xc_pair(half, pair):
+            return xc[half][:].rearrange("p (c i) t -> p c t i", i=RUN)[:, :, 2 * pair : 2 * pair + 2, :]
+
+        wide = [keep.tile([P, 2, 2 * HALF], F32, name="wide%d" % kind) for kind in range(3)]
+        for t in range(2):
+            for kind in range(3):
+                gather(wide[kind][:, t, :], kind, t, slice(0, 2 * LIST_COLS))
+        wide_capped = keep.tile([P, 2, 2 * HALF], F32, name="wide_capped")
+        nc.vector.tensor_tensor(wide_capped[:], wide[0][:], wide[1][:], ALU.min)
+        for half in range(2):
+            slots = slice(half * HALF, (half + 1) * HALF)
+            nc.vector.tensor_tensor(
+                xc_pair(half, 0), by_runs(wide_capped[:, :, slots]), by_runs(wide[2][:, :, slots]), ALU.max
+            )
+
         for half in range(2):
             cols = slice(half * LIST_COLS, (half + 1) * LIST_COLS)
-            code = keep.tile([P, PACK, HALF], F32, name="code%d" % half, tag="code")
-            upper = keep.tile([P, PACK, HALF], F32, name="upper%d" % half, tag="upper")
-            lower = keep.tile([P, PACK, HALF], F32, name="lower%d" % half, tag="lower")
-            gathers = [(t, kind) for t in range(PACK) for kind in range(3)]
+            picked = [keep.tile([P, 2, HALF], F32, name="picked%d_%d" % (half, kind), tag="picked%d" % kind) for kind in range(3)]
+            order = [(t, kind) for t in range(2) for kind in range(3)]
             if half == 1:
-                gathers = [(t, kind) for kind in range(3) for t in range(PACK)]
-            for t, kind in gathers:
-                dst, rows, offsets, step = [
-                    (code, ta_rows, list_a, step_a),
-                    (upper, tb_rows, list_upper, step_upper),
-                    (lower, tb_rows, list_lower, step_lower),
-                ][kind]
-                nc.scalar.activation(
-                    out=dst[:, t, :], in_=rows[t][:].indirect(offsets[:, cols]), func=COPY, scale=step[:, t : t + 1]
-                )
-
-            capped = keep.tile([P, PACK, HALF], F32, name="capped%d" % half, tag="capped0" if half == 0 else "hidden0", align_bytes=64)
-            xc = keep.tile([P, HALF, PACK], BF16, name="xc%d" % half, tag="xc", align_bytes=64)
-            xc_runs = xc[:].rearrange("p (c i) t -> p c t i", i=RUN)
+                order = [(t, kind) for kind in range(3) for t in range(2)]
+            for t, kind in order:
+                gather(picked[kind][:, t, :], kind, 2 + t, cols)
+            capped = keep.tile([P, 2, HALF], F32, name="capped%d" % half, tag="capped0" if half == 0 else "vs_table", align_bytes=64)
             if half == 0:
-                nc.vector.tensor_tensor(capped[:, :LAST, :], code[:, :LAST, :], upper[:, :LAST, :], ALU.min)
-                nc.vector.tensor_tensor(
-                    xc_runs[:, :, :LAST, :], by_runs(capped[:, :LAST, :]), by_runs(lower[:, :LAST, :]), ALU.max
-                )
-                nc.vector.tensor_tensor(capped[:, LAST, :], code[:, LAST, :], upper[:, LAST, :], ALU.min)
-                nc.vector.tensor_tensor(xc[:, :, LAST], capped[:, LAST, :], lower[:, LAST, :], ALU.max)
+                for t in range(2):
+                    nc.vector.tensor_tensor(capped[:, t, :], picked[0][:, t, :], picked[1][:, t, :], ALU.min)
             else:
-                nc.vector.tensor_tensor(capped[:], code[:], upper[:], ALU.min)
-                nc.vector.tensor_tensor(xc_runs, by_runs(capped[:]), by_runs(lower[:]), ALU.max)
+                nc.vector.tensor_tensor(capped[:], picked[0][:], picked[1][:], ALU.min)
+            nc.vector.tensor_tensor(xc_pair(half, 1), by_runs(capped[:]), by_runs(picked[2][:]), ALU.max)
 
             xc_words = keep.tile([P, HALF], U32, name="xc_words%d" % half, align_bytes=64)
             xc_plane = keep.tile([P, HALF], U8, name="xc_plane%d" % half, align_bytes=64)
             nc.vector.quantize_mx(
-                out=xc_words[:].bitcast(FP8X4), scales=xc_plane[:], in_=xc[:].rearrange("p j t -> p (j t)")
+                out=xc_words[:].bitcast(FP8X4), scales=xc_plane[:], in_=xc[half][:].rearrange("p j t -> p (j t)")
             )
+            if half == 0:
+                vs_picked = keep.tile([P, OUT_ROWS], U32, name="vs_picked", tag="xc0", align_bytes=64)
+                nc.vector.tensor_copy(vs_picked[:], vs_table[:].bitcast(U32).indirect(list_store[:]))
 
             first_bank = psum.tile([P, HALF], F32, name="first_bank%d" % half)
             rest_bank = psum.tile([P, LAST, HALF], F32, name="rest_bank%d" % half)
@@ -160,7 +184,7 @@ def tile_picked_boundedcode_plain_one_boardpair_store_plain_kernel(
                     start=True,
                     stop=True,
                 )
-            hidden = keep.tile([P, PACK, HALF], F32, name="hidden%d" % half, tag="hidden%d" % half, align_bytes=64)
+            hidden = keep.tile([P, PACK, HALF], F32, name="hidden%d" % half, align_bytes=64)
             if half == 0:
                 nc.vector.tensor_copy(hidden[:, 0, :], first_bank[:])
             else:
@@ -169,8 +193,8 @@ def tile_picked_boundedcode_plain_one_boardpair_store_plain_kernel(
             for t in range(PACK):
                 nc.vector.tensor_copy(board[t][:].indirect(list_board[:, cols]), hidden[:, t, :])
 
-        vs_picked = keep.tile([P, OUT_ROWS], U32, name="vs_picked", tag="xc", align_bytes=64)
-        nc.vector.tensor_copy(vs_picked[:], vs_table[:].bitcast(U32).indirect(list_store[:]))
+        vs_plane_picked = keep.tile([P, OUT_ROWS], U8, name="vs_plane_picked", tag="hidden1", align_bytes=64)
+        nc.vector.tensor_copy(vs_plane_picked[:], vs_plane[:].indirect(list_store[:]))
 
         first = keep.tile([P, PACK, PLACES], F32, name="first")
         second = keep.tile([P, PACK, PLACES], F32, name="second")
@@ -185,8 +209,11 @@ def tile_picked_boundedcode_plain_one_boardpair_store_plain_kernel(
         hid = keep.tile([P, PLACES, PACK], BF16, name="hid", align_bytes=64)
         for rows in (slice(0, LAST), slice(LAST, PACK)):
             nc.vector.tensor_tensor(gap[:, rows, :], first[:, rows, :], second[:, rows, :], ALU.subtract)
-            gap_by_place = gap[:, rows, :].rearrange("p t o -> p o t")
-            nc.vector.scalar_tensor_tensor(hid[:, :, rows], gap_by_place, -1.0, gap_by_place, ALU.mult, ALU.max)
+        gap_by_place = gap[:].rearrange("p t o -> p o t")
+        nc.scalar.activation(out=hid[:, :, 0:2], in_=gap_by_place[:, :, 0:2], func=ABS)
+        nc.vector.scalar_tensor_tensor(
+            hid[:, :, 2:4], gap_by_place[:, :, 2:4], -1.0, gap_by_place[:, :, 2:4], ALU.mult, ALU.max
+        )
         hid_words = keep.tile([P, PLACES], U32, name="hid_words", align_bytes=64)
         hid_plane = keep.tile([P, PLACES], U8, name="hid_plane", align_bytes=64)
         nc.vector.quantize_mx(

from contextlib import ExitStack

import concourse.mybir as mybir

FLOPS = 167772160

F32 = mybir.dt.float32
BF16 = mybir.dt.bfloat16
I32 = mybir.dt.int32
U32 = mybir.dt.uint32
U16 = mybir.dt.uint16
U8 = mybir.dt.uint8
FP8X4 = mybir.dt.float8_e4m3fn_x4
FP4X4 = mybir.dt.float4_e2m1fn_x4
ALU = mybir.AluOpType
COPY = mybir.ActivationFunctionType.Copy
ABS = mybir.ActivationFunctionType.Abs

P = 128
PACK = 4
LAST = PACK - 1
TABLE = 512
HALF = 128
LIST_COLS = HALF // 16
BOARD = 512
PLACES = 128
HIDDEN = 512
STORE = 1024
OUT_ROWS = 256
RUN = 4


def tile_picked_boundedcode_plain_one_boardpair_store_plain_kernel(
    tc, ta, tb, ga, gb, gd, w_words, w_scales, sa, sb, vs_words, vs_scales,
    offs, offs2, offs3, offs4, offs5, offs6, offs7, out,
):
    nc = tc.nc
    with ExitStack() as ctx:
        lists = ctx.enter_context(tc.tile_pool(name="lists", bufs=1))
        keep = ctx.enter_context(tc.tile_pool(name="keep", bufs=1))
        psum = ctx.enter_context(tc.psum_pool(name="psum", bufs=1))

        def load_list(src, name):
            tile = lists.tile(list(src.shape), U16, name=name)
            nc.sync.dma_start(tile[:], src)
            return tile

        def load_factor(src, name):
            tile = keep.tile([P, PACK], F32, name=name)
            nc.sync.dma_start(tile[:], src.rearrange("(p t) o -> p (t o)", t=PACK))
            return tile

        def load_rows(src, t, name):
            tile = keep.tile([P, TABLE], F32, name=name)
            nc.sync.dma_start(tile[:], src.rearrange("(p t) c -> t p c", t=PACK)[t])
            return tile

        def load_scale_plane(src, width, name):
            staged = keep.tile([PACK, PACK, width // 4], I32, name=name + "_staged")
            nc.sync.dma_start(staged[:], src[0].bitcast(I32).rearrange("(q i) c -> i q c", i=PACK))
            plane = keep.tile([P, width], U8, name=name, align_bytes=64)
            nc.vector.memset(plane[:].bitcast(I32), 0)
            for q in range(PACK):
                nc.vector.tensor_copy(plane[:].bitcast(I32)[32 * q : 32 * q + PACK, :], staged[:, q, :])
            return plane

        warm_in = keep.tile([P, 1], F32, name="warm_in")
        warm_out = keep.tile([P, 1], F32, name="warm_out")
        nc.vector.memset(warm_in[:], 0.0)
        nc.scalar.activation(out=warm_out[:], in_=warm_in[:], func=COPY)

        vs_plane = keep.tile([P, STORE], U8, name="vs_plane", align_bytes=64)
        nc.vector.memset(vs_plane[:].bitcast(I32), 0)
        ta_rows = [load_rows(ta, 0, "ta0")]
        list_a = load_list(offs, "list_a")
        step_a = load_factor(ga, "step_a")
        list_upper = load_list(offs2, "list_upper")
        step_upper = load_factor(gb, "step_upper")
        tb_rows = [load_rows(tb, 0, "tb0")]
        ta_rows.append(load_rows(ta, 1, "ta1"))
        tb_rows.append(load_rows(tb, 1, "tb1"))
        list_lower = load_list(offs3, "list_lower")
        step_lower = load_factor(gd, "step_lower")
        w_plane = load_scale_plane(w_scales, HIDDEN, "w_plane")
        ta_rows.append(load_rows(ta, 2, "ta2"))
        tb_rows.append(load_rows(tb, 2, "tb2"))
        w_raw = keep.tile([P, 2 * HIDDEN], U8, name="w_raw")
        nc.sync.dma_start(w_raw[:].bitcast(I32), w_words[0].bitcast(I32))
        ta_rows.append(load_rows(ta, 3, "ta3"))
        tb_rows.append(load_rows(tb, 3, "tb3"))
        list_store = load_list(offs7, "list_store")
        vs_table = keep.tile([P, STORE], I32, name="vs_table", tag="vs_table", align_bytes=64)
        nc.sync.dma_start(vs_table[:], vs_words[0].rearrange("p n t -> p (n t)").bitcast(I32))
        for q in range(PACK):
            nc.sync.dma_start(
                vs_plane[:].bitcast(I32)[32 * q : 32 * q + PACK, :], vs_scales[0].bitcast(I32)[PACK * q : PACK * (q + 1), :]
            )
        list_first = load_list(offs5, "list_first")
        weight_first = load_factor(sa, "weight_first")
        list_second = load_list(offs6, "list_second")
        weight_second = load_factor(sb, "weight_second")
        list_board = load_list(offs4, "list_board")


        board = [keep.tile([P, BOARD], F32, name="board%d" % t) for t in range(PACK)]
        for t in range(PACK):
            nc.vector.memset(board[t][:], 0.0)

        w_dealt = keep.tile([P, 2 * HIDDEN], U8, name="w_dealt", align_bytes=64)
        nc.vector.tensor_copy(
            w_dealt[:].bitcast(U16).rearrange("p (t m) -> p t m", t=PACK),
            w_raw[:].bitcast(U16).rearrange("p (m t) -> p t m", t=PACK),
        )
        w_plane_dealt = keep.tile([P, HIDDEN], U8, name="w_plane_dealt", align_bytes=64)
        nc.vector.tensor_copy(
            w_plane_dealt[:].rearrange("p (t m) -> p t m", t=PACK),
            w_plane[:].rearrange("p (m t) -> p t m", t=PACK),
        )

        def by_runs(rows):
            return rows.rearrange("p t (c i) -> p c t i", i=RUN)

        def gather(dst, kind, t, cols):
            rows, offsets, step = [
                (ta_rows, list_a, step_a),
                (tb_rows, list_upper, step_upper),
                (tb_rows, list_lower, step_lower),
            ][kind]
            nc.scalar.activation(
                out=dst, in_=rows[t][:].indirect(offsets[:, cols]), func=COPY, scale=step[:, t : t + 1]
            )

        xc = [keep.tile([P, HALF, PACK], BF16, name="xc%d" % half, align_bytes=64) for half in range(2)]

        def xc_pair(half, pair):
            return xc[half][:].rearrange("p (c i) t -> p c t i", i=RUN)[:, :, 2 * pair : 2 * pair + 2, :]

        wide = [keep.tile([P, 2, 2 * HALF], F32, name="wide%d" % kind) for kind in range(3)]
        for t in range(2):
            for kind in range(3):
                gather(wide[kind][:, t, :], kind, t, slice(0, 2 * LIST_COLS))
        wide_capped = keep.tile([P, 2, 2 * HALF], F32, name="wide_capped")
        nc.vector.tensor_tensor(wide_capped[:], wide[0][:], wide[1][:], ALU.min)
        for half in range(2):
            slots = slice(half * HALF, (half + 1) * HALF)
            nc.vector.tensor_tensor(
                xc_pair(half, 0), by_runs(wide_capped[:, :, slots]), by_runs(wide[2][:, :, slots]), ALU.max
            )

        for half in range(2):
            cols = slice(half * LIST_COLS, (half + 1) * LIST_COLS)
            picked = [keep.tile([P, 2, HALF], F32, name="picked%d_%d" % (half, kind), tag="picked%d" % kind) for kind in range(3)]
            order = [(t, kind) for t in range(2) for kind in range(3)]
            if half == 1:
                order = [(t, kind) for kind in range(3) for t in range(2)]
            for t, kind in order:
                gather(picked[kind][:, t, :], kind, 2 + t, cols)
            capped = keep.tile([P, 2, HALF], F32, name="capped%d" % half, tag="capped0" if half == 0 else "vs_table", align_bytes=64)
            if half == 0:
                for t in range(2):
                    nc.vector.tensor_tensor(capped[:, t, :], picked[0][:, t, :], picked[1][:, t, :], ALU.min)
            else:
                nc.vector.tensor_tensor(capped[:], picked[0][:], picked[1][:], ALU.min)
            nc.vector.tensor_tensor(xc_pair(half, 1), by_runs(capped[:]), by_runs(picked[2][:]), ALU.max)

            xc_words = keep.tile([P, HALF], U32, name="xc_words%d" % half, align_bytes=64)
            xc_plane = keep.tile([P, HALF], U8, name="xc_plane%d" % half, align_bytes=64)
            nc.vector.quantize_mx(
                out=xc_words[:].bitcast(FP8X4), scales=xc_plane[:], in_=xc[half][:].rearrange("p j t -> p (j t)")
            )
            if half == 0:
                vs_picked = keep.tile([P, OUT_ROWS], U32, name="vs_picked", tag="xc0", align_bytes=64)
                nc.vector.tensor_copy(vs_picked[:], vs_table[:].bitcast(U32).indirect(list_store[:]))

            first_bank = psum.tile([P, HALF], F32, name="first_bank%d" % half)
            rest_bank = psum.tile([P, LAST, HALF], F32, name="rest_bank%d" % half)
            for t in range(PACK):
                nc.tensor.matmul_mx(
                    out=first_bank[:] if t == 0 else rest_bank[:, t - 1, :],
                    lhsT=w_dealt[:, 2 * P * t : 2 * P * (t + 1)].bitcast(FP4X4),
                    lhsT_scale=w_plane_dealt[:, P * t : P * (t + 1)],
                    rhs=xc_words[:].bitcast(FP8X4),
                    rhs_scale=xc_plane[:],
                    start=True,
                    stop=True,
                )
            hidden = keep.tile([P, PACK, HALF], F32, name="hidden%d" % half, align_bytes=64)
            if half == 0:
                nc.vector.tensor_copy(hidden[:, 0, :], first_bank[:])
            else:
                nc.scalar.copy(hidden[:, 0, :], first_bank[:])
            nc.scalar.copy(hidden[:, 1:, :], rest_bank[:])
            for t in range(PACK):
                nc.vector.tensor_copy(board[t][:].indirect(list_board[:, cols]), hidden[:, t, :])

        vs_plane_picked = keep.tile([P, OUT_ROWS], U8, name="vs_plane_picked", tag="hidden1", align_bytes=64)
        nc.vector.tensor_copy(vs_plane_picked[:], vs_plane[:].indirect(list_store[:]))

        first = keep.tile([P, PACK, PLACES], F32, name="first")
        second = keep.tile([P, PACK, PLACES], F32, name="second")
        for t in range(PACK):
            nc.scalar.activation(
                out=first[:, t, :], in_=board[t][:].indirect(list_first[:]), func=COPY, scale=weight_first[:, t : t + 1]
            )
            nc.scalar.activation(
                out=second[:, t, :], in_=board[t][:].indirect(list_second[:]), func=COPY, scale=weight_second[:, t : t + 1]
            )
        gap = keep.tile([P, PACK, PLACES], F32, name="gap")
        hid = keep.tile([P, PLACES, PACK], BF16, name="hid", align_bytes=64)
        for rows in (slice(0, LAST), slice(LAST, PACK)):
            nc.vector.tensor_tensor(gap[:, rows, :], first[:, rows, :], second[:, rows, :], ALU.subtract)
        gap_by_place = gap[:].rearrange("p t o -> p o t")
        nc.scalar.activation(out=hid[:, :, 0:2], in_=gap_by_place[:, :, 0:2], func=ABS)
        nc.vector.scalar_tensor_tensor(
            hid[:, :, 2:4], gap_by_place[:, :, 2:4], -1.0, gap_by_place[:, :, 2:4], ALU.mult, ALU.max
        )
        hid_words = keep.tile([P, PLACES], U32, name="hid_words", align_bytes=64)
        hid_plane = keep.tile([P, PLACES], U8, name="hid_plane", align_bytes=64)
        nc.vector.quantize_mx(
            out=hid_words[:].bitcast(FP8X4), scales=hid_plane[:], in_=hid[:].rearrange("p o t -> p (o t)")
        )

        for b in range(OUT_ROWS // P):
            rows = slice(b * P, (b + 1) * P)
            bank = psum.tile([P, PLACES], F32, name="out_bank%d" % b)
            nc.tensor.matmul_mx(
                out=bank[:],
                lhsT=vs_picked[:, rows].bitcast(FP8X4),
                lhsT_scale=vs_plane_picked[:, rows],
                rhs=hid_words[:].bitcast(FP8X4),
                rhs_scale=hid_plane[:],
                start=True,
                stop=True,
            )
            result = keep.tile([P, PLACES], F32, name="result%d" % b)
            if b == 0:
                nc.scalar.copy(result[:], bank[:])
                nc.scalar.dma_start(out[rows, :], result[:])
            else:
                nc.vector.tensor_copy(result[:], bank[:])
                nc.sync.dma_start(out[rows, :], result[:])
